import numpy as np
import ml_dtypes


def mxq(x, axis, fmt="e4m3"):
    dtype, down = {"e4m3": (ml_dtypes.float8_e4m3fn, 7), "e5m2": (ml_dtypes.float8_e5m2, 14)}[fmt]
    v = np.moveaxis(np.asarray(x, np.float32).astype(ml_dtypes.bfloat16).astype(np.float64), axis, -1)
    blocks = v.reshape(v.shape[:-1] + (-1, 32))
    amax = np.abs(blocks).max(-1, keepdims=True)
    byte = np.maximum(np.where(amax > 0, np.frexp(amax)[1] - 1 + 127, 0) - down, 1)
    scale = np.exp2(byte - 127.0)
    codes = (blocks / scale).astype(np.float32).astype(dtype).astype(np.float64)
    return np.moveaxis((codes * scale).reshape(v.shape), -1, axis)


WIDE = False


def mx_kscale(k):
    if not WIDE:
        return np.ones(k)
    levels = np.array([10, -10, 5, -5, 0])
    if k % 512:
        return np.exp2(np.random.permutation(np.resize(levels, k // 32))).repeat(32)
    a = np.empty((k // 512, 16))
    for p in range(k // 512):
        a[p, :8] = np.random.permutation(np.resize(levels, 8))
        for g in range(8):
            far = levels[np.abs(levels - a[p, g]) >= 10]
            a[p, g + 8] = far[np.random.randint(len(far))]
    return np.exp2(a.ravel()).repeat(32)


def f64(x):
    return np.asarray(x).astype(np.float64)


def striped(idx):
    return np.tile(idx.reshape(-1, 16).T, (8, 1)).astype(np.uint16)


def unstriped(offs):
    return offs[:16].T.reshape(-1).astype(np.int64)


E2M1 = np.array([0.0, 0.5, 1.0, 1.5, 2.0, 3.0, 4.0, 6.0, -0.0, -0.5, -1.0, -1.5, -2.0, -3.0, -4.0, -6.0])


def pack_weight(w, fmt):
    k, n = w.shape
    w = f64(np.asarray(w, np.float32).astype(ml_dtypes.bfloat16)).reshape(k // 32, 32, n)
    amax = np.abs(w).max(1)
    if fmt == "e4m3":
        byte = np.frexp(amax)[1] - 1 + 127 - 7
    else:
        mant, ex = np.frexp(amax / 6.0)
        byte = np.where(mant > 0.5, ex, ex - 1) + 127
    byte = np.clip(np.where(amax > 0, byte, 1), 1, 254)
    scaled = (w * np.exp2(127.0 - byte)[:, None, :]).reshape(k, n).astype(np.float32)
    by_word = np.ascontiguousarray(scaled.reshape(k // 512, 128, 4, n).transpose(0, 1, 3, 2))
    if fmt == "e4m3":
        words = by_word.astype(ml_dtypes.float8_e4m3fn).view(np.uint8)
    else:
        c = by_word.astype(ml_dtypes.float4_e2m1fn).view(np.uint8) & 0xF
        words = (c[..., 0::2] | (c[..., 1::2] << 4)).reshape(k // 512, 128, 2 * n)
    return np.ascontiguousarray(words), np.ascontiguousarray(byte.astype(np.uint8).reshape(k // 512, 16, n))


def unpack_weight(words, scales, fmt):
    g, _, n = scales.shape
    words = np.ascontiguousarray(words).reshape(g, 128, n, -1)
    if fmt == "e4m3":
        vals = words.view(ml_dtypes.float8_e4m3fn).astype(np.float64)
    else:
        nib = np.empty((g, 128, n, 4), np.uint8)
        nib[..., 0::2] = words & 0xF
        nib[..., 1::2] = words >> 4
        vals = E2M1[nib]
    vals = vals * np.repeat(np.exp2(scales.astype(np.float64) - 127.0), 8, axis=1)[..., None]
    return vals.transpose(0, 1, 3, 2).reshape(g * 512, n)


def gelu(v):
    return 0.5 * v * (1.0 + np.tanh(np.sqrt(2.0 / np.pi) * (v + 0.044715 * v**3)))


K, T, S, P, H, N = 1024, 4096, 1024, 512, 512, 768

def setup_inputs():
    n = np.random.standard_normal
    s = mx_kscale(K)[:, None]
    u = mx_kscale(H)[:, None]
    perm = np.random.permutation(S)
    tab_words, tab_scales = pack_weight(n((K, T)) * s, "e4m3")
    w2_words, w2_scales = pack_weight(0.8 * n((K, H)) / np.sqrt(K) / s, "e2m1")
    return {
        "tab_words": tab_words, "tab_scales": tab_scales,
        "offs": striped(np.random.permutation(T)[:S]),
        "pos1": striped(perm[:P]),
        "pos2": striped(perm[P:]),
        "w1": (0.8 * n((K, H)) / np.sqrt(K) / s).astype(np.float32),
        "w2_words": w2_words, "w2_scales": w2_scales,
        "temp": np.random.uniform(0.4, 1.6, H).astype(np.float32),
        "drift": (3.5 * n((H, P))).astype(np.float32),
        "lift": (0.6 * n(H)).astype(np.float32),
        "trim": (0.7 * n(H)).astype(np.float32),
        "wgs": np.exp(0.3 * n((128, P))).astype(np.float32),
        "gain": (np.random.uniform(0.5, 1.5, H) * u[:, 0]).astype(np.float32),
        "w3": (n((H, N)) / np.sqrt(H) / u).astype(np.float32),
        "chan": np.random.uniform(0.5, 1.5, N).astype(np.float32),
        "ref0": (0.7 * n((N, S))).astype(np.float32),
    }

def reference(tab_words, tab_scales, offs, pos1, pos2, w1, w2_words, w2_scales, temp, drift, lift, trim, wgs, gain, w3, chan, ref0):
    v = unpack_weight(tab_words, tab_scales, "e4m3")[:, unstriped(offs)]
    w2 = unpack_weight(w2_words, w2_scales, "e2m1")
    h = np.maximum(mxq(f64(w1), 0, "e4m3").T @ v, w2.T @ v)
    top = h.max(axis=1)
    a = np.exp(f64(temp)[:, None] * (h[:, unstriped(pos1)] - top[:, None]))
    a = a * f64(drift) + f64(lift)[:, None]
    page = h + f64(trim)[:, None]
    page[:, unstriped(pos2)] = np.tile(f64(wgs), (H // 128, 1)) * a
    q = mxq(page * f64(gain)[:, None], 0, "e4m3")
    y = mxq(f64(w3), 0, "e4m3").T @ q
    return y * f64(chan)[:, None] + f64(ref0)

@@ -1,0 +1,283 @@
+from contextlib import ExitStack
+
+import concourse.mybir as mybir
+
+K, T, S, LOOKS, H, N = 1024, 4096, 1024, 512, 512, 768
+FLOPS = 2 * (2 * K * H * S) + 2 * H * N * S
+
+F32 = mybir.dt.float32
+BF16 = mybir.dt.bfloat16
+I32 = mybir.dt.int32
+U32 = mybir.dt.uint32
+U16 = mybir.dt.uint16
+U8 = mybir.dt.uint8
+FP8X4 = mybir.dt.float8_e4m3fn_x4
+FP4X4 = mybir.dt.float4_e2m1fn_x4
+ACT = mybir.ActivationFunctionType
+ALU = mybir.AluOpType
+
+P = 128
+PACK = 4
+PASSES = K // (P * PACK)
+BANK = 512
+HALVES = S // BANK
+N_TILES = N // P
+CHUNKS = ((0, 256), (256, 512), (512, 1024))
+
+
+def tile_list_tape_flutter_readout_kernel(
+    tc, tab_words, tab_scales, offs, pos1, pos2, w1, w2_words, w2_scales,
+    temp, drift, lift, trim, wgs, gain, w3, chan, ref0, out,
+):
+    nc = tc.nc
+    with ExitStack() as ctx:
+        sb = ctx.enter_context(tc.tile_pool(name="sb", bufs=1))
+        ps = ctx.enter_context(tc.psum_pool(name="ps", bufs=4))
+
+        def tile(name, shape, dtype, tag=None):
+            return sb.tile(shape, dtype, name=name, tag=tag or name, align_bytes=64)
+
+        def load_rows(name, vec):
+            rows = tile(name, [P, PACK], F32)
+            nc.sync.dma_start(rows[:], vec.rearrange("(p t) -> p t", t=PACK))
+            return rows
+
+        tab_s = tile("tab_s", [P, T], U8)
+        nc.vector.memset(tab_s[32:64, :].bitcast(I32), 0)
+        nc.vector.memset(tab_s[64:128, :].bitcast(I32), 0)
+        v_s = tile("v_s", [P, PASSES * S], U8)
+        nc.vector.memset(v_s[:].bitcast(I32), 0)
+        w2s_raw = tile("w2s_raw", [P, PASSES * H], U8)
+        nc.gpsimd.memset(w2s_raw[:].bitcast(I32), 0)
+        for q in range(4):
+            nc.gpsimd.dma_start(
+                w2s_raw[32 * q : 32 * q + 4, :].bitcast(I32).rearrange("p (a w) -> p a w", a=PASSES),
+                w2_scales[:, 4 * q : 4 * q + 4, :].rearrange("a r c -> r a c").bitcast(I32),
+            )
+
+        offs_t = tile("offs_t", [P, S // 16], U16)
+        nc.sync.dma_start(offs_t[:], offs)
+        nc.sync.dma_start(tab_s[0:32, :].bitcast(I32), tab_scales.rearrange("a q t -> (a q) t").bitcast(I32))
+        tab_w = [tile("tab_w%d" % a, [P, T], I32) for a in range(PASSES)]
+        nc.sync.dma_start(tab_w[0][:], tab_words[0].rearrange("p t i -> p (t i)").bitcast(I32))
+        w2w_raw = tile("w2w_raw", [P, PASSES * 2 * H], U8)
+        nc.sync.dma_start(
+            w2w_raw[:].bitcast(I32).rearrange("p (a w) -> p a w", a=PASSES),
+            w2_words.rearrange("a p b -> p a b").bitcast(I32),
+        )
+        w1_rows = w1.rearrange("(a p j) c -> a p j c", a=PASSES, j=PACK)
+        w1_first = tile("w1_first", [P, PACK, H], F32)
+        nc.sync.dma_start(w1_first[:], w1_rows[0])
+        nc.sync.dma_start(tab_w[1][:], tab_words[1].rearrange("p t i -> p (t i)").bitcast(I32))
+        w1_last = [tile("w1_last%d" % u, [P, PACK, H // 2], F32) for u in range(2)]
+        for u in range(2):
+            nc.sync.dma_start(w1_last[u][:], w1_rows[1][:, :, u * (H // 2) : (u + 1) * (H // 2)])
+        trim_t = load_rows("trim_t", trim)
+        temp_t = load_rows("temp_t", temp)
+        pos1_t = tile("pos1_t", [P, LOOKS // 16], U16)
+        nc.sync.dma_start(pos1_t[:], pos1)
+        drift_t = tile("drift_t", [P, PACK, LOOKS], F32)
+        nc.sync.dma_start(drift_t[:], drift.rearrange("(p t) m -> p t m", t=PACK))
+        lift_t = load_rows("lift_t", lift)
+        pos2_t = tile("pos2_t", [P, LOOKS // 16], U16)
+        nc.sync.dma_start(pos2_t[:], pos2)
+        wgs_t = tile("wgs_t", [P, PACK, LOOKS], F32)
+        for q in range(4):
+            nc.sync.dma_start(wgs_t[32 * q : 32 * q + 32], wgs.rearrange("(p t) m -> p t m", t=PACK))
+        gain_t = load_rows("gain_t", gain)
+        w3_raw = tile("w3_raw", [P, PACK, N], F32)
+        nc.sync.dma_start(w3_raw[:], w3.rearrange("(p t) n -> p t n", t=PACK))
+        chan_t = tile("chan_t", [P, N_TILES], F32)
+        with nc.allow_non_contiguous_dma(reason="one value a partition and output tile"):
+            nc.sync.dma_start(chan_t[:], chan.rearrange("(c p) -> p c", p=P))
+        res = tile("res", [P, N_TILES, S], F32)
+        nc.sync.dma_start(res[:], ref0.rearrange("(c p) j -> p c j", p=P))
+
+        w2w = tile("w2w", [P, PASSES * 2 * H], U8)
+        nc.scalar.copy(
+            w2w[:].bitcast(U16).rearrange("p (a t m) -> p a m t", a=PASSES, t=PACK),
+            w2w_raw[:].bitcast(U16).rearrange("p (a m t) -> p a m t", a=PASSES, t=PACK),
+        )
+        neg_temp = tile("neg_temp", [P, PACK], F32)
+        nc.gpsimd.tensor_scalar(neg_temp[:], temp_t[:], -1.0, 0.0, ALU.mult, ALU.add)
+        temp_trim = tile("temp_trim", [P, PACK], F32)
+        nc.gpsimd.tensor_tensor(temp_trim[:], temp_t[:], trim_t[:], ALU.mult)
+
+        v_w = [tile("v_w%d" % a, [P, S], U32) for a in range(PASSES)]
+        w1_bf = [tile("w1_bf%d" % a, [P, PACK * H], BF16) for a in range(PASSES)]
+        w1_w = [tile("w1_w%d" % a, [P, H], U32) for a in range(PASSES)]
+        w1_s = [tile("w1_s%d" % a, [P, H], U8) for a in range(PASSES)]
+
+        def dealt(a):
+            return w1_bf[a][:].rearrange("p (t m j) -> p m j t", t=PACK, j=PACK)
+
+        def quantise_w1(a, lo, hi):
+            nc.vector.quantize_mx(
+                out=w1_w[a][:, lo:hi].bitcast(FP8X4), scales=w1_s[a][:, lo:hi],
+                in_=w1_bf[a][:, PACK * lo : PACK * hi],
+            )
+
+        picked_s = tile("picked_s", [P, S], U8)
+        nc.vector.tensor_copy(picked_s[:], tab_s[:].indirect(offs_t[:]))
+        for a in range(PASSES):
+            for q in range(4):
+                nc.gpsimd.dma_start(
+                    v_s[32 * q : 32 * q + 4, a * S : (a + 1) * S].bitcast(I32),
+                    picked_s[16 * a + 4 * q : 16 * a + 4 * q + 4, :].bitcast(I32),
+                )
+        w2s = tile("w2s", [P, PASSES * H], U8)
+        nc.vector.tensor_copy(
+            w2s[:].rearrange("p (a t m) -> p a m t", a=PASSES, t=PACK),
+            w2s_raw[:].rearrange("p (a m t) -> p a m t", a=PASSES, t=PACK),
+        )
+        nc.vector.tensor_copy(v_w[0][:], tab_w[0][:].bitcast(U32).indirect(offs_t[:]))
+        nc.scalar.copy(dealt(0), w1_first[:].rearrange("p j (m t) -> p m j t", t=PACK))
+        quantise_w1(0, 0, H)
+        for u in range(HALVES):
+            nc.vector.tensor_copy(
+                v_w[1][:, u * BANK : (u + 1) * BANK],
+                tab_w[1][:].bitcast(U32).indirect(offs_t[:, u * (BANK // 16) : (u + 1) * (BANK // 16)]),
+            )
+        for u in range(2):
+            nc.vector.tensor_copy(
+                dealt(1)[:, u * (P // 2) : (u + 1) * (P // 2)],
+                w1_last[u][:].rearrange("p j (m t) -> p m j t", t=PACK),
+            )
+        quantise_w1(1, 0, P)
+        quantise_w1(1, P, H)
+
+        def mm_w2(acc, t, u, a):
+            cols = slice(u * BANK, (u + 1) * BANK)
+            nc.tensor.matmul_mx(
+                out=acc[:],
+                lhsT=w2w[:, a * 2 * H + 2 * P * t : a * 2 * H + 2 * P * (t + 1)].bitcast(FP4X4),
+                lhsT_scale=w2s[:, a * H + P * t : a * H + P * (t + 1)],
+                rhs=v_w[a][:, cols].bitcast(FP8X4), rhs_scale=v_s[:, a * S + u * BANK : a * S + (u + 1) * BANK],
+                start=(a == 0), stop=(a == PASSES - 1),
+            )
+
+        def mm_w1(acc, t, u, a):
+            cols = slice(u * BANK, (u + 1) * BANK)
+            nc.tensor.matmul_mx(
+                out=acc[:],
+                lhsT=w1_w[a][:, P * t : P * (t + 1)].bitcast(FP8X4),
+                lhsT_scale=w1_s[a][:, P * t : P * (t + 1)],
+                rhs=v_w[a][:, cols].bitcast(FP8X4), rhs_scale=v_s[:, a * S + u * BANK : a * S + (u + 1) * BANK],
+                start=(a == 0), stop=(a == PASSES - 1),
+            )
+
+        h2 = [[tile("h2_%d_%d" % (t, u), [P, BANK], F32) for u in range(HALVES)] for t in range(PACK)]
+        h = [tile("h_%d" % t, [P, S], F32) for t in range(PACK)]
+        page = [tile("page_%d" % t, [P, S], F32) for t in range(PACK)]
+        look = [tile("look_%d" % t, [P, LOOKS], F32) for t in range(PACK)]
+        drifted, put = {}, {}
+        page_top = tile("page_top", [P, PACK], F32)
+        look_bias = tile("look_bias", [P, PACK], F32)
+
+        def second_reading(t):
+            for u in range(HALVES):
+                acc = ps.tile([P, BANK], F32, name="acc2", tag="second")
+                for a in range(PASSES):
+                    mm_w2(acc, t, u, a)
+                nc.scalar.copy(h2[t][u][:], acc[:])
+
+        def features(t):
+            for u in range(HALVES):
+                cols = slice(u * BANK, (u + 1) * BANK)
+                acc = ps.tile([P, BANK], F32, name="acc1", tag="first")
+                for a in range(PASSES):
+                    mm_w1(acc, t, u, a)
+                nc.vector.tensor_tensor(h[t][:, cols], acc[:], h2[t][u][:], ALU.max)
+
+        def page_and_look(t):
+            col = slice(t, t + 1)
+            nc.vector.tensor_scalar(
+                page[t][:], h[t][:], trim_t[:, col], None, ALU.add, ALU.max, accum_out=page_top[:, col]
+            )
+            nc.scalar.activation(
+                look_bias[:, col], page_top[:, col], ACT.Identity, bias=temp_trim[:, col], scale=neg_temp[:, col]
+            )
+            nc.scalar.activation(
+                look[t][:], h[t][:].indirect(pos1_t[:]), ACT.Exp, bias=look_bias[:, col], scale=temp_t[:, col]
+            )
+
+        def times_drift(t, tag=None):
+            drifted[t] = tile("drifted_%d" % t, [P, LOOKS], F32, tag)
+            nc.vector.tensor_tensor(drifted[t][:], look[t][:], drift_t[:, t, :], ALU.mult)
+
+        def plus_lift(t, tag=None):
+            put[t] = tile("put_%d" % t, [P, LOOKS], F32, tag)
+            nc.scalar.activation(put[t][:], drifted[t][:], ACT.Identity, bias=lift_t[:, t : t + 1])
+
+        def scatter(t):
+            nc.vector.tensor_tensor(page[t][:].indirect(pos2_t[:]), put[t][:], wgs_t[:, t, :], ALU.mult)
+
+        def round_page(t, lo, hi):
+            nc.scalar.activation(q_bf[:, lo:hi, t], page[t][:, lo:hi], ACT.Copy, scale=gain_t[:, t : t + 1])
+
+        w3_w = tile("w3_w", [P, N], U32)
+        w3_s = tile("w3_s", [P, N], U8)
+
+        def prepare_w3(lo, hi, tag):
+            w3_bf = tile("w3_bf%d" % lo, [P, (hi - lo) * PACK], BF16, tag)
+            nc.scalar.copy(
+                w3_bf[:].rearrange("p (c i t) -> p c t i", i=4, t=PACK),
+                w3_raw[:, :, lo:hi].rearrange("p t (c i) -> p c t i", i=4),
+            )
+            nc.vector.quantize_mx(out=w3_w[:, lo:hi].bitcast(FP8X4), scales=w3_s[:, lo:hi], in_=w3_bf[:])
+
+        second_reading(0)
+        second_reading(1)
+        features(0)
+        second_reading(2)
+        page_and_look(0)
+        features(1)
+        second_reading(3)
+        page_and_look(1)
+        times_drift(0, "h2_0_0")
+        features(2)
+        page_and_look(2)
+        features(3)
+        plus_lift(0, "h2_3_1")
+        page_and_look(3)
+        prepare_w3(0, 256, "h_2")
+        times_drift(1, "h2_3_0")
+        times_drift(2, "h2_0_1")
+        plus_lift(2, "h2_1_1")
+        scatter(0)
+        times_drift(3)
+        put[1] = tile("put_1", [P, LOOKS], F32, "look_3")
+        nc.vector.tensor_scalar(put[1][:], drifted[1][:], lift_t[:, 1:2], None, ALU.add)
+        prepare_w3(256, N, "h_3")
+        plus_lift(3, "w3_raw")
+        q_bf = tile("q_bf", [P, S, PACK], BF16, "drifted_3")
+        round_page(0, 0, S)
+        scatter(1)
+        round_page(1, 0, S)
+        scatter(2)
+        round_page(2, 0, S)
+        scatter(3)
+
+        out_rows = out.rearrange("(c p) j -> p c j", p=P)
+        for i, (lo, hi) in enumerate(CHUNKS):
+            round_page(PACK - 1, lo, hi)
+            q_w = tile("q_w%d" % i, [P, hi - lo], U32, "q_w%d" % (i % 2))
+            q_s = tile("q_s%d" % i, [P, hi - lo], U8, "q_s%d" % (i % 2))
+            nc.vector.quantize_mx(
+                out=q_w[:].bitcast(FP8X4), scales=q_s[:],
+                in_=q_bf[:, lo:hi, :].rearrange("p j t -> p (j t)"),
+            )
+            for c in range(N_TILES):
+                acc = ps.tile([P, BANK], F32, name="acc3", tag="first" if c % 2 == 0 else "second")
+                nc.tensor.matmul_mx(
+                    out=acc[:, : hi - lo],
+                    lhsT=w3_w[:, P * c : P * (c + 1)].bitcast(FP8X4), lhsT_scale=w3_s[:, P * c : P * (c + 1)],
+                    rhs=q_w[:].bitcast(FP8X4), rhs_scale=q_s[:],
+                    start=True, stop=True,
+                )
+                nc.vector.scalar_tensor_tensor(
+                    res[:, c, lo:hi], acc[:, : hi - lo], chan_t[:, c : c + 1], res[:, c, lo:hi], ALU.mult, ALU.add
+                )
+                step = 2 if hi - lo < BANK else 1
+                if (c + 1) % step == 0:
+                    nc.sync.dma_start(out_rows[:, c + 1 - step : c + 1, lo:hi], res[:, c + 1 - step : c + 1, lo:hi])

@@ -32,7 +32,7 @@ def tile_list_tape_flutter_readout_kernel(
     nc = tc.nc
     with ExitStack() as ctx:
         sb = ctx.enter_context(tc.tile_pool(name="sb", bufs=1))
-        ps = ctx.enter_context(tc.psum_pool(name="ps", bufs=4))
+        ps = ctx.enter_context(tc.psum_pool(name="ps", bufs=1))
 
         def tile(name, shape, dtype, tag=None):
             return sb.tile(shape, dtype, name=name, tag=tag or name, align_bytes=64)
@@ -82,34 +82,33 @@ def tile_list_tape_flutter_readout_kernel(
         pos2_t = tile("pos2_t", [P, LOOKS // 16], U16)
         nc.sync.dma_start(pos2_t[:], pos2)
         wgs_t = tile("wgs_t", [P, PACK, LOOKS], F32)
-        for q in range(4):
+        for q in (0, 2, 1, 3):
             nc.sync.dma_start(wgs_t[32 * q : 32 * q + 32], wgs.rearrange("(p t) m -> p t m", t=PACK))
         gain_t = load_rows("gain_t", gain)
         w3_raw = tile("w3_raw", [P, PACK, N], F32)
         nc.sync.dma_start(w3_raw[:], w3.rearrange("(p t) n -> p t n", t=PACK))
+        res = tile("res", [P, N_TILES, S], F32)
+        nc.sync.dma_start(res[:], ref0.rearrange("(c p) j -> p c j", p=P))
         chan_t = tile("chan_t", [P, N_TILES], F32)
         with nc.allow_non_contiguous_dma(reason="one value a partition and output tile"):
             nc.sync.dma_start(chan_t[:], chan.rearrange("(c p) -> p c", p=P))
-        res = tile("res", [P, N_TILES, S], F32)
-        nc.sync.dma_start(res[:], ref0.rearrange("(c p) j -> p c j", p=P))
 
         w2w = tile("w2w", [P, PASSES * 2 * H], U8)
         nc.scalar.copy(
-            w2w[:].bitcast(U16).rearrange("p (a t m) -> p a m t", a=PASSES, t=PACK),
-            w2w_raw[:].bitcast(U16).rearrange("p (a m t) -> p a m t", a=PASSES, t=PACK),
+            w2w[:].bitcast(U16).rearrange("p (a t m) -> p a t m", a=PASSES, t=PACK),
+            w2w_raw[:].bitcast(U16).rearrange("p (a m t) -> p a t m", a=PASSES, t=PACK),
         )
         neg_temp = tile("neg_temp", [P, PACK], F32)
         nc.gpsimd.tensor_scalar(neg_temp[:], temp_t[:], -1.0, 0.0, ALU.mult, ALU.add)
-        temp_trim = tile("temp_trim", [P, PACK], F32)
-        nc.gpsimd.tensor_tensor(temp_trim[:], temp_t[:], trim_t[:], ALU.mult)
 
         v_w = [tile("v_w%d" % a, [P, S], U32) for a in range(PASSES)]
         w1_bf = [tile("w1_bf%d" % a, [P, PACK * H], BF16) for a in range(PASSES)]
         w1_w = [tile("w1_w%d" % a, [P, H], U32) for a in range(PASSES)]
         w1_s = [tile("w1_s%d" % a, [P, H], U8) for a in range(PASSES)]
 
-        def dealt(a):
-            return w1_bf[a][:].rearrange("p (t m j) -> p m j t", t=PACK, j=PACK)
+        def round_w1(copy, a, raw, places, slices):
+            dealt = w1_bf[a][:].rearrange("p (t m j) -> p t m j", t=PACK, j=PACK)
+            copy(dealt[:, slices, places], raw[:].rearrange("p j (m t) -> p t m j", t=PACK)[:, slices])
 
         def quantise_w1(a, lo, hi):
             nc.vector.quantize_mx(
@@ -125,26 +124,23 @@ def tile_list_tape_flutter_readout_kernel(
                     v_s[32 * q : 32 * q + 4, a * S : (a + 1) * S].bitcast(I32),
                     picked_s[16 * a + 4 * q : 16 * a + 4 * q + 4, :].bitcast(I32),
                 )
+        nc.vector.tensor_copy(v_w[0][:], tab_w[0][:].bitcast(U32).indirect(offs_t[:]))
         w2s = tile("w2s", [P, PASSES * H], U8)
         nc.vector.tensor_copy(
-            w2s[:].rearrange("p (a t m) -> p a m t", a=PASSES, t=PACK),
-            w2s_raw[:].rearrange("p (a m t) -> p a m t", a=PASSES, t=PACK),
+            w2s[:].rearrange("p (a t m) -> p a t m", a=PASSES, t=PACK),
+            w2s_raw[:].rearrange("p (a m t) -> p a t m", a=PASSES, t=PACK),
         )
-        nc.vector.tensor_copy(v_w[0][:], tab_w[0][:].bitcast(U32).indirect(offs_t[:]))
-        nc.scalar.copy(dealt(0), w1_first[:].rearrange("p j (m t) -> p m j t", t=PACK))
+        round_w1(nc.scalar.copy, 0, w1_first, slice(0, P), slice(0, PACK))
         quantise_w1(0, 0, H)
         for u in range(HALVES):
             nc.vector.tensor_copy(
                 v_w[1][:, u * BANK : (u + 1) * BANK],
                 tab_w[1][:].bitcast(U32).indirect(offs_t[:, u * (BANK // 16) : (u + 1) * (BANK // 16)]),
             )
-        for u in range(2):
-            nc.vector.tensor_copy(
-                dealt(1)[:, u * (P // 2) : (u + 1) * (P // 2)],
-                w1_last[u][:].rearrange("p j (m t) -> p m j t", t=PACK),
-            )
-        quantise_w1(1, 0, P)
-        quantise_w1(1, P, H)
+        for slices in (slice(0, 1), slice(1, PACK)):
+            round_w1(nc.scalar.copy, 1, w1_last[0], slice(0, P // 2), slices)
+            round_w1(nc.vector.tensor_copy, 1, w1_last[1], slice(P // 2, P), slices)
+            quantise_w1(1, P * slices.start, P * slices.stop)
 
         def mm_w2(acc, t, u, a):
             cols = slice(u * BANK, (u + 1) * BANK)
@@ -156,17 +152,19 @@ def tile_list_tape_flutter_readout_kernel(
                 start=(a == 0), stop=(a == PASSES - 1),
             )
 
-        def mm_w1(acc, t, u, a):
+        def mm_w1(acc, t, u, a, order):
             cols = slice(u * BANK, (u + 1) * BANK)
             nc.tensor.matmul_mx(
                 out=acc[:],
                 lhsT=w1_w[a][:, P * t : P * (t + 1)].bitcast(FP8X4),
                 lhsT_scale=w1_s[a][:, P * t : P * (t + 1)],
                 rhs=v_w[a][:, cols].bitcast(FP8X4), rhs_scale=v_s[:, a * S + u * BANK : a * S + (u + 1) * BANK],
-                start=(a == 0), stop=(a == PASSES - 1),
+                start=(a == order[0]), stop=(a == order[-1]),
             )
 
-        h2 = [[tile("h2_%d_%d" % (t, u), [P, BANK], F32) for u in range(HALVES)] for t in range(PACK)]
+        h2_early = tile("h2_early", [P, 2 * HALVES, BANK], F32, "w1_last0")
+        h2 = [[h2_early[:, HALVES * t + u, :] for u in range(HALVES)] for t in range(2)]
+        h2 = h2 + [[tile("h2_%d_%d" % (t, u), [P, BANK], F32)[:] for u in range(HALVES)] for t in range(2, PACK)]
         h = [tile("h_%d" % t, [P, S], F32) for t in range(PACK)]
         page = [tile("page_%d" % t, [P, S], F32) for t in range(PACK)]
         look = [tile("look_%d" % t, [P, LOOKS], F32) for t in range(PACK)]
@@ -176,34 +174,35 @@ def tile_list_tape_flutter_readout_kernel(
 
         def second_reading(t):
             for u in range(HALVES):
-                acc = ps.tile([P, BANK], F32, name="acc2", tag="second")
+                acc = ps.tile([P, BANK], F32, name="acc2", tag="bank%d" % ((0, 2, 4, 6)[t] + u))
                 for a in range(PASSES):
                     mm_w2(acc, t, u, a)
-                nc.scalar.copy(h2[t][u][:], acc[:])
+                nc.scalar.copy(h2[t][u], acc[:])
 
         def features(t):
             for u in range(HALVES):
                 cols = slice(u * BANK, (u + 1) * BANK)
-                acc = ps.tile([P, BANK], F32, name="acc1", tag="first")
-                for a in range(PASSES):
-                    mm_w1(acc, t, u, a)
-                nc.vector.tensor_tensor(h[t][:, cols], acc[:], h2[t][u][:], ALU.max)
+                acc = ps.tile([P, BANK], F32, name="acc1", tag="bank%d" % ((4, 6, 0, 2)[t] + u))
+                order = (0, 1) if t < 2 else (1, 0)
+                for a in order:
+                    mm_w1(acc, t, u, a, order)
+                nc.vector.tensor_tensor(h[t][:, cols], acc[:], h2[t][u], ALU.max)
 
         def page_and_look(t):
             col = slice(t, t + 1)
             nc.vector.tensor_scalar(
                 page[t][:], h[t][:], trim_t[:, col], None, ALU.add, ALU.max, accum_out=page_top[:, col]
             )
-            nc.scalar.activation(
-                look_bias[:, col], page_top[:, col], ACT.Identity, bias=temp_trim[:, col], scale=neg_temp[:, col]
+            nc.vector.tensor_scalar(
+                look_bias[:, col], page_top[:, col], trim_t[:, col], neg_temp[:, col], ALU.subtract, ALU.mult
             )
             nc.scalar.activation(
                 look[t][:], h[t][:].indirect(pos1_t[:]), ACT.Exp, bias=look_bias[:, col], scale=temp_t[:, col]
             )
 
-        def times_drift(t, tag=None):
+        def times_drift(engine, t, tag=None):
             drifted[t] = tile("drifted_%d" % t, [P, LOOKS], F32, tag)
-            nc.vector.tensor_tensor(drifted[t][:], look[t][:], drift_t[:, t, :], ALU.mult)
+            engine.tensor_tensor(drifted[t][:], look[t][:], drift_t[:, t, :], ALU.mult)
 
         def plus_lift(t, tag=None):
             put[t] = tile("put_%d" % t, [P, LOOKS], F32, tag)
@@ -215,15 +214,17 @@ def tile_list_tape_flutter_readout_kernel(
         def round_page(t, lo, hi):
             nc.scalar.activation(q_bf[:, lo:hi, t], page[t][:, lo:hi], ACT.Copy, scale=gain_t[:, t : t + 1])
 
-        w3_w = tile("w3_w", [P, N], U32)
         w3_s = tile("w3_s", [P, N], U8)
 
-        def prepare_w3(lo, hi, tag):
+        def round_w3(lo, hi, tag):
             w3_bf = tile("w3_bf%d" % lo, [P, (hi - lo) * PACK], BF16, tag)
             nc.scalar.copy(
                 w3_bf[:].rearrange("p (c i t) -> p c t i", i=4, t=PACK),
                 w3_raw[:, :, lo:hi].rearrange("p t (c i) -> p c t i", i=4),
             )
+            return w3_bf
+
+        def quantise_w3(lo, hi, w3_bf):
             nc.vector.quantize_mx(out=w3_w[:, lo:hi].bitcast(FP8X4), scales=w3_s[:, lo:hi], in_=w3_bf[:])
 
         second_reading(0)
@@ -234,21 +235,25 @@ def tile_list_tape_flutter_readout_kernel(
         features(1)
         second_reading(3)
         page_and_look(1)
-        times_drift(0, "h2_0_0")
+        times_drift(nc.gpsimd, 0)
+        times_drift(nc.gpsimd, 1)
         features(2)
         page_and_look(2)
         features(3)
-        plus_lift(0, "h2_3_1")
+        put[0] = tile("put_0", [P, LOOKS], F32, "h2_3_1")
+        nc.gpsimd.tensor_scalar(put[0][:], drifted[0][:], lift_t[:, 0:1], 1.0, ALU.add, ALU.mult)
         page_and_look(3)
-        prepare_w3(0, 256, "h_2")
-        times_drift(1, "h2_3_0")
-        times_drift(2, "h2_0_1")
-        plus_lift(2, "h2_1_1")
+        w3_low = round_w3(0, 256, "h_2")
+        times_drift(nc.vector, 2, "w1_first")
+        plus_lift(2, "w1_last1")
         scatter(0)
-        times_drift(3)
+        times_drift(nc.vector, 3)
         put[1] = tile("put_1", [P, LOOKS], F32, "look_3")
         nc.vector.tensor_scalar(put[1][:], drifted[1][:], lift_t[:, 1:2], None, ALU.add)
-        prepare_w3(256, N, "h_3")
+        w3_high = round_w3(256, N, "h_3")
+        w3_w = tile("w3_w", [P, N], U32, "h2_3_1")
+        quantise_w3(0, 256, w3_low)
+        quantise_w3(256, N, w3_high)
         plus_lift(3, "w3_raw")
         q_bf = tile("q_bf", [P, S, PACK], BF16, "drifted_3")
         round_page(0, 0, S)
@@ -268,7 +273,7 @@ def tile_list_tape_flutter_readout_kernel(
                 in_=q_bf[:, lo:hi, :].rearrange("p j t -> p (j t)"),
             )
             for c in range(N_TILES):
-                acc = ps.tile([P, BANK], F32, name="acc3", tag="first" if c % 2 == 0 else "second")
+                acc = ps.tile([P, BANK], F32, name="acc3", tag="bank%d" % ((N_TILES * i + c) % 8))
                 nc.tensor.matmul_mx(
                     out=acc[:, : hi - lo],
                     lhsT=w3_w[:, P * c : P * (c + 1)].bitcast(FP8X4), lhsT_scale=w3_s[:, P * c : P * (c + 1)],

from contextlib import ExitStack

import concourse.mybir as mybir

K, T, S, LOOKS, H, N = 1024, 4096, 1024, 512, 512, 768
FLOPS = 2 * (2 * K * H * S) + 2 * H * N * S

F32 = mybir.dt.float32
BF16 = mybir.dt.bfloat16
I32 = mybir.dt.int32
U32 = mybir.dt.uint32
U16 = mybir.dt.uint16
U8 = mybir.dt.uint8
FP8X4 = mybir.dt.float8_e4m3fn_x4
FP4X4 = mybir.dt.float4_e2m1fn_x4
ACT = mybir.ActivationFunctionType
ALU = mybir.AluOpType

P = 128
PACK = 4
PASSES = K // (P * PACK)
BANK = 512
HALVES = S // BANK
N_TILES = N // P
CHUNKS = ((0, 256), (256, 512), (512, 1024))


def tile_list_tape_flutter_readout_kernel(
    tc, tab_words, tab_scales, offs, pos1, pos2, w1, w2_words, w2_scales,
    temp, drift, lift, trim, wgs, gain, w3, chan, ref0, out,
):
    nc = tc.nc
    with ExitStack() as ctx:
        sb = ctx.enter_context(tc.tile_pool(name="sb", bufs=1))
        ps = ctx.enter_context(tc.psum_pool(name="ps", bufs=1))

        def tile(name, shape, dtype, tag=None):
            return sb.tile(shape, dtype, name=name, tag=tag or name, align_bytes=64)

        def load_rows(name, vec):
            rows = tile(name, [P, PACK], F32)
            nc.sync.dma_start(rows[:], vec.rearrange("(p t) -> p t", t=PACK))
            return rows

        tab_s = tile("tab_s", [P, T], U8)
        nc.vector.memset(tab_s[32:64, :].bitcast(I32), 0)
        nc.vector.memset(tab_s[64:128, :].bitcast(I32), 0)
        v_s = tile("v_s", [P, PASSES * S], U8)
        nc.vector.memset(v_s[:].bitcast(I32), 0)
        w2s_raw = tile("w2s_raw", [P, PASSES * H], U8)
        nc.gpsimd.memset(w2s_raw[:].bitcast(I32), 0)
        for q in range(4):
            nc.gpsimd.dma_start(
                w2s_raw[32 * q : 32 * q + 4, :].bitcast(I32).rearrange("p (a w) -> p a w", a=PASSES),
                w2_scales[:, 4 * q : 4 * q + 4, :].rearrange("a r c -> r a c").bitcast(I32),
            )

        offs_t = tile("offs_t", [P, S // 16], U16)
        nc.sync.dma_start(offs_t[:], offs)
        nc.sync.dma_start(tab_s[0:32, :].bitcast(I32), tab_scales.rearrange("a q t -> (a q) t").bitcast(I32))
        tab_w = [tile("tab_w%d" % a, [P, T], I32) for a in range(PASSES)]
        nc.sync.dma_start(tab_w[0][:], tab_words[0].rearrange("p t i -> p (t i)").bitcast(I32))
        w2w_raw = tile("w2w_raw", [P, PASSES * 2 * H], U8)
        nc.sync.dma_start(
            w2w_raw[:].bitcast(I32).rearrange("p (a w) -> p a w", a=PASSES),
            w2_words.rearrange("a p b -> p a b").bitcast(I32),
        )
        w1_rows = w1.rearrange("(a p j) c -> a p j c", a=PASSES, j=PACK)
        w1_first = tile("w1_first", [P, PACK, H], F32)
        nc.sync.dma_start(w1_first[:], w1_rows[0])
        nc.sync.dma_start(tab_w[1][:], tab_words[1].rearrange("p t i -> p (t i)").bitcast(I32))
        w1_last = [tile("w1_last%d" % u, [P, PACK, H // 2], F32) for u in range(2)]
        for u in range(2):
            nc.sync.dma_start(w1_last[u][:], w1_rows[1][:, :, u * (H // 2) : (u + 1) * (H // 2)])
        trim_t = load_rows("trim_t", trim)
        temp_t = load_rows("temp_t", temp)
        pos1_t = tile("pos1_t", [P, LOOKS // 16], U16)
        nc.sync.dma_start(pos1_t[:], pos1)
        drift_t = tile("drift_t", [P, PACK, LOOKS], F32)
        nc.sync.dma_start(drift_t[:], drift.rearrange("(p t) m -> p t m", t=PACK))
        lift_t = load_rows("lift_t", lift)
        pos2_t = tile("pos2_t", [P, LOOKS // 16], U16)
        nc.sync.dma_start(pos2_t[:], pos2)
        wgs_t = tile("wgs_t", [P, PACK, LOOKS], F32)
        for q in (0, 2, 1, 3):
            nc.sync.dma_start(wgs_t[32 * q : 32 * q + 32], wgs.rearrange("(p t) m -> p t m", t=PACK))
        gain_t = load_rows("gain_t", gain)
        w3_raw = tile("w3_raw", [P, PACK, N], F32)
        nc.sync.dma_start(w3_raw[:], w3.rearrange("(p t) n -> p t n", t=PACK))
        res = tile("res", [P, N_TILES, S], F32)
        nc.sync.dma_start(res[:], ref0.rearrange("(c p) j -> p c j", p=P))
        chan_t = tile("chan_t", [P, N_TILES], F32)
        with nc.allow_non_contiguous_dma(reason="one value a partition and output tile"):
            nc.sync.dma_start(chan_t[:], chan.rearrange("(c p) -> p c", p=P))

        w2w = tile("w2w", [P, PASSES * 2 * H], U8)
        nc.scalar.copy(
            w2w[:].bitcast(U16).rearrange("p (a t m) -> p a t m", a=PASSES, t=PACK),
            w2w_raw[:].bitcast(U16).rearrange("p (a m t) -> p a t m", a=PASSES, t=PACK),
        )
        neg_temp = tile("neg_temp", [P, PACK], F32)
        nc.gpsimd.tensor_scalar(neg_temp[:], temp_t[:], -1.0, 0.0, ALU.mult, ALU.add)

        v_w = [tile("v_w%d" % a, [P, S], U32) for a in range(PASSES)]
        w1_bf = [tile("w1_bf%d" % a, [P, PACK * H], BF16) for a in range(PASSES)]
        w1_w = [tile("w1_w%d" % a, [P, H], U32) for a in range(PASSES)]
        w1_s = [tile("w1_s%d" % a, [P, H], U8) for a in range(PASSES)]

        def round_w1(copy, a, raw, places, slices):
            dealt = w1_bf[a][:].rearrange("p (t m j) -> p t m j", t=PACK, j=PACK)
            copy(dealt[:, slices, places], raw[:].rearrange("p j (m t) -> p t m j", t=PACK)[:, slices])

        def quantise_w1(a, lo, hi):
            nc.vector.quantize_mx(
                out=w1_w[a][:, lo:hi].bitcast(FP8X4), scales=w1_s[a][:, lo:hi],
                in_=w1_bf[a][:, PACK * lo : PACK * hi],
            )

        picked_s = tile("picked_s", [P, S], U8)
        nc.vector.tensor_copy(picked_s[:], tab_s[:].indirect(offs_t[:]))
        for a in range(PASSES):
            for q in range(4):
                nc.gpsimd.dma_start(
                    v_s[32 * q : 32 * q + 4, a * S : (a + 1) * S].bitcast(I32),
                    picked_s[16 * a + 4 * q : 16 * a + 4 * q + 4, :].bitcast(I32),
                )
        nc.vector.tensor_copy(v_w[0][:], tab_w[0][:].bitcast(U32).indirect(offs_t[:]))
        w2s = tile("w2s", [P, PASSES * H], U8)
        nc.vector.tensor_copy(
            w2s[:].rearrange("p (a t m) -> p a t m", a=PASSES, t=PACK),
            w2s_raw[:].rearrange("p (a m t) -> p a t m", a=PASSES, t=PACK),
        )
        round_w1(nc.scalar.copy, 0, w1_first, slice(0, P), slice(0, PACK))
        quantise_w1(0, 0, H)
        for u in range(HALVES):
            nc.vector.tensor_copy(
                v_w[1][:, u * BANK : (u + 1) * BANK],
                tab_w[1][:].bitcast(U32).indirect(offs_t[:, u * (BANK // 16) : (u + 1) * (BANK // 16)]),
            )
        for slices in (slice(0, 1), slice(1, PACK)):
            round_w1(nc.scalar.copy, 1, w1_last[0], slice(0, P // 2), slices)
            round_w1(nc.vector.tensor_copy, 1, w1_last[1], slice(P // 2, P), slices)
            quantise_w1(1, P * slices.start, P * slices.stop)

        def mm_w2(acc, t, u, a):
            cols = slice(u * BANK, (u + 1) * BANK)
            nc.tensor.matmul_mx(
                out=acc[:],
                lhsT=w2w[:, a * 2 * H + 2 * P * t : a * 2 * H + 2 * P * (t + 1)].bitcast(FP4X4),
                lhsT_scale=w2s[:, a * H + P * t : a * H + P * (t + 1)],
                rhs=v_w[a][:, cols].bitcast(FP8X4), rhs_scale=v_s[:, a * S + u * BANK : a * S + (u + 1) * BANK],
                start=(a == 0), stop=(a == PASSES - 1),
            )

        def mm_w1(acc, t, u, a, order):
            cols = slice(u * BANK, (u + 1) * BANK)
            nc.tensor.matmul_mx(
                out=acc[:],
                lhsT=w1_w[a][:, P * t : P * (t + 1)].bitcast(FP8X4),
                lhsT_scale=w1_s[a][:, P * t : P * (t + 1)],
                rhs=v_w[a][:, cols].bitcast(FP8X4), rhs_scale=v_s[:, a * S + u * BANK : a * S + (u + 1) * BANK],
                start=(a == order[0]), stop=(a == order[-1]),
            )

        h2_early = tile("h2_early", [P, 2 * HALVES, BANK], F32, "w1_last0")
        h2 = [[h2_early[:, HALVES * t + u, :] for u in range(HALVES)] for t in range(2)]
        h2 = h2 + [[tile("h2_%d_%d" % (t, u), [P, BANK], F32)[:] for u in range(HALVES)] for t in range(2, PACK)]
        h = [tile("h_%d" % t, [P, S], F32) for t in range(PACK)]
        page = [tile("page_%d" % t, [P, S], F32) for t in range(PACK)]
        look = [tile("look_%d" % t, [P, LOOKS], F32) for t in range(PACK)]
        drifted, put = {}, {}
        page_top = tile("page_top", [P, PACK], F32)
        look_bias = tile("look_bias", [P, PACK], F32)

        def second_reading(t):
            for u in range(HALVES):
                acc = ps.tile([P, BANK], F32, name="acc2", tag="bank%d" % ((0, 2, 4, 6)[t] + u))
                for a in range(PASSES):
                    mm_w2(acc, t, u, a)
                nc.scalar.copy(h2[t][u], acc[:])

        def features(t):
            for u in range(HALVES):
                cols = slice(u * BANK, (u + 1) * BANK)
                acc = ps.tile([P, BANK], F32, name="acc1", tag="bank%d" % ((4, 6, 0, 2)[t] + u))
                order = (0, 1) if t < 2 else (1, 0)
                for a in order:
                    mm_w1(acc, t, u, a, order)
                nc.vector.tensor_tensor(h[t][:, cols], acc[:], h2[t][u], ALU.max)

        def page_and_look(t):
            col = slice(t, t + 1)
            nc.vector.tensor_scalar(
                page[t][:], h[t][:], trim_t[:, col], None, ALU.add, ALU.max, accum_out=page_top[:, col]
            )
            nc.vector.tensor_scalar(
                look_bias[:, col], page_top[:, col], trim_t[:, col], neg_temp[:, col], ALU.subtract, ALU.mult
            )
            nc.scalar.activation(
                look[t][:], h[t][:].indirect(pos1_t[:]), ACT.Exp, bias=look_bias[:, col], scale=temp_t[:, col]
            )

        def times_drift(engine, t, tag=None):
            drifted[t] = tile("drifted_%d" % t, [P, LOOKS], F32, tag)
            engine.tensor_tensor(drifted[t][:], look[t][:], drift_t[:, t, :], ALU.mult)

        def plus_lift(t, tag=None):
            put[t] = tile("put_%d" % t, [P, LOOKS], F32, tag)
            nc.scalar.activation(put[t][:], drifted[t][:], ACT.Identity, bias=lift_t[:, t : t + 1])

        def scatter(t):
            nc.vector.tensor_tensor(page[t][:].indirect(pos2_t[:]), put[t][:], wgs_t[:, t, :], ALU.mult)

        def round_page(t, lo, hi):
            nc.scalar.activation(q_bf[:, lo:hi, t], page[t][:, lo:hi], ACT.Copy, scale=gain_t[:, t : t + 1])

        w3_s = tile("w3_s", [P, N], U8)

        def round_w3(lo, hi, tag):
            w3_bf = tile("w3_bf%d" % lo, [P, (hi - lo) * PACK], BF16, tag)
            nc.scalar.copy(
                w3_bf[:].rearrange("p (c i t) -> p c t i", i=4, t=PACK),
                w3_raw[:, :, lo:hi].rearrange("p t (c i) -> p c t i", i=4),
            )
            return w3_bf

        def quantise_w3(lo, hi, w3_bf):
            nc.vector.quantize_mx(out=w3_w[:, lo:hi].bitcast(FP8X4), scales=w3_s[:, lo:hi], in_=w3_bf[:])

        second_reading(0)
        second_reading(1)
        features(0)
        second_reading(2)
        page_and_look(0)
        features(1)
        second_reading(3)
        page_and_look(1)
        times_drift(nc.gpsimd, 0)
        times_drift(nc.gpsimd, 1)
        features(2)
        page_and_look(2)
        features(3)
        put[0] = tile("put_0", [P, LOOKS], F32, "h2_3_1")
        nc.gpsimd.tensor_scalar(put[0][:], drifted[0][:], lift_t[:, 0:1], 1.0, ALU.add, ALU.mult)
        page_and_look(3)
        w3_low = round_w3(0, 256, "h_2")
        times_drift(nc.vector, 2, "w1_first")
        plus_lift(2, "w1_last1")
        scatter(0)
        times_drift(nc.vector, 3)
        put[1] = tile("put_1", [P, LOOKS], F32, "look_3")
        nc.vector.tensor_scalar(put[1][:], drifted[1][:], lift_t[:, 1:2], None, ALU.add)
        w3_high = round_w3(256, N, "h_3")
        w3_w = tile("w3_w", [P, N], U32, "h2_3_1")
        quantise_w3(0, 256, w3_low)
        quantise_w3(256, N, w3_high)
        plus_lift(3, "w3_raw")
        q_bf = tile("q_bf", [P, S, PACK], BF16, "drifted_3")
        round_page(0, 0, S)
        scatter(1)
        round_page(1, 0, S)
        scatter(2)
        round_page(2, 0, S)
        scatter(3)

        out_rows = out.rearrange("(c p) j -> p c j", p=P)
        for i, (lo, hi) in enumerate(CHUNKS):
            round_page(PACK - 1, lo, hi)
            q_w = tile("q_w%d" % i, [P, hi - lo], U32, "q_w%d" % (i % 2))
            q_s = tile("q_s%d" % i, [P, hi - lo], U8, "q_s%d" % (i % 2))
            nc.vector.quantize_mx(
                out=q_w[:].bitcast(FP8X4), scales=q_s[:],
                in_=q_bf[:, lo:hi, :].rearrange("p j t -> p (j t)"),
            )
            for c in range(N_TILES):
                acc = ps.tile([P, BANK], F32, name="acc3", tag="bank%d" % ((N_TILES * i + c) % 8))
                nc.tensor.matmul_mx(
                    out=acc[:, : hi - lo],
                    lhsT=w3_w[:, P * c : P * (c + 1)].bitcast(FP8X4), lhsT_scale=w3_s[:, P * c : P * (c + 1)],
                    rhs=q_w[:].bitcast(FP8X4), rhs_scale=q_s[:],
                    start=True, stop=True,
                )
                nc.vector.scalar_tensor_tensor(
                    res[:, c, lo:hi], acc[:, : hi - lo], chan_t[:, c : c + 1], res[:, c, lo:hi], ALU.mult, ALU.add
                )
                step = 2 if hi - lo < BANK else 1
                if (c + 1) % step == 0:
                    nc.sync.dma_start(out_rows[:, c + 1 - step : c + 1, lo:hi], res[:, c + 1 - step : c + 1, lo:hi])
